import numpy as np, ml_dtypes
CORES = [24,25,26,27,28,29,30,31,224,225,226,227,228,229,230,231]
N = 16
WB, KB, QP = 2, 1, 128
WID = [64,48,16,128,112,128,16,64,128,128,16,16,64,128,128,16]
def setup_inputs(rng):
    return {"q": rng.standard_normal((N, 128, QP), dtype=np.float32).astype(ml_dtypes.bfloat16), "k": rng.standard_normal((N, 128, KB * 128), dtype=np.float32).astype(ml_dtypes.bfloat16), "v": rng.standard_normal((N, 128, KB * 128), dtype=np.float32).astype(ml_dtypes.bfloat16)}
def setup_inputs_big(rng):
    d = setup_inputs(rng)
    for k in ("q", "k", "v"): d[k] = (d[k].astype(np.float32) * 1024.0).astype(d[k].dtype)
    return d
def setup_inputs_small(rng):
    d = setup_inputs(rng)
    for k in ("q", "k", "v"): d[k] = (d[k].astype(np.float32) * (1 / 1024.0)).astype(d[k].dtype)
    return d
def setup_inputs_apart(rng):
    d = setup_inputs(rng)
    f = (10.0 ** rng.permutation(np.linspace(-1.5, 1.5, N))).astype(np.float32).reshape(N, 1, 1)
    for k in ("q", "k", "v"): d[k] = (d[k].astype(np.float32) * f).astype(d[k].dtype)
    return d
def whole(q, k, v):
    Q, K, V = q.astype(np.float64), k.astype(np.float64), v.astype(np.float64)
    y = np.zeros((N, 128, QP))
    for r in range(N):
        for j in range(max(0, r - WB), r + 1):
            for b in range(KB):
                S = np.maximum(K[j][:, 128 * b:128 * b + 128].T @ Q[r], 0.0)
                y[r] += V[j][:, 128 * b:128 * b + 128].T @ S
    return {"y": y.astype(ml_dtypes.bfloat16 if q.dtype != np.float64 else np.float64)}
def reference(q, k, v):
    o = whole(q, k, v)["y"].copy()
    for r in range(N):
        o[r][:, WID[r]:] = np.nan
    return {"y": o}

@@ -1,0 +1,128 @@
+from concourse.bass import DstId, RemoteDMATransfer
+from concourse.mybir import AluOpType
+
+P = 128
+WINDOW = 2
+ENGINES = 8
+
+SCRATCH = {
+    "kv": ("sbuf", [P, 2 * P], "bfloat16"),
+    "ld0": ("sbuf", [P, 2 * P], "bfloat16"),
+    "ld1": ("sbuf", [P, 2 * P], "bfloat16"),
+    "qs": ("sbuf", [P, P], "bfloat16"),
+    "zero": ("sbuf", [P, P], "float32"),
+    "s0": ("sbuf", [P, P], "bfloat16"),
+    "s1": ("sbuf", [P, P], "bfloat16"),
+    "s2": ("sbuf", [P, P], "bfloat16"),
+    "ys": ("sbuf", [P, P], "bfloat16"),
+    "p0": ("psum", [P, 512], "float32"),
+    "p1": ("psum", [P, 512], "float32"),
+    "p2": ("psum", [P, 512], "float32"),
+    "po": ("psum", [P, 512], "float32"),
+}
+SEMAPHORES = ["ldkv", "ldq", "arr0", "arr1", "sent", "zf", "m0", "m1", "m2", "r0", "r1", "r2", "od", "cp", "st"]
+
+
+def _low(mask, n):
+    out, b = 0, 1
+    while n and b <= mask:
+        if mask & b:
+            out |= b
+            n -= 1
+        b <<= 1
+    return out
+
+
+def _bits(mask):
+    return bin(mask).count("1")
+
+
+def _near(topo, a, b):
+    return (topo.host(a), topo.chip(a)) == (topo.host(b), topo.chip(b))
+
+
+def _calls(j, cores, topo):
+    src = cores[j]
+    dests = [d for d in range(j + 1, j + 1 + WINDOW) if d < len(cores)]
+    far = [d for d in dests if not _near(topo, src, cores[d])]
+    near = [d for d in dests if _near(topo, src, cores[d])]
+    out, used = [], 0
+    for group in (far, near):
+        if not group:
+            continue
+        allowed = topo.mask(src, cores[group[0]])
+        for d in group:
+            assert topo.may_write(src, cores[d])
+            allowed &= topo.mask(src, cores[d])
+        free = allowed & ~used
+        m = _low(free if _bits(free) >= ENGINES else allowed, ENGINES)
+        used |= m
+        out.append((m, group))
+    return out
+
+
+def rank_program(g, core, T, topo):
+    r = T.rank_of(core)
+    if r is None:
+        return
+    cores, sem = T.cores, T.sem
+    W = T.tables["WID"][r]
+
+    g.sync.dma_start(T.kv[:, 0:P], T.k[:, :]).then_inc(sem.ldkv, 16)
+    g.scalar.dma_start(T.kv[:, P:2 * P], T.v[:, :]).then_inc(sem.ldkv, 16)
+    g.sync.dma_start(T.qs[:, 0:W], T.q[:, 0:W]).then_inc(sem.ldq, 16)
+
+    calls = _calls(r, cores, topo)
+    if calls:
+        g.wait_ge(sem.ldkv, 32)
+        left = 0
+        for m, group in calls:
+            ids = []
+            for d in group:
+                rid, pid = topo.addr(cores[d], core)
+                ids.append(DstId(rid=rid, pnc=pid))
+            g.remote_dma_fused(
+                [RemoteDMATransfer(dst_ids=ids, dma_engine_mask=m, remote_sem=sem["arr%d" % (r % 2)],
+                                   srcs=[T.kv[:]], dsts=[T["ld%d" % (r % 2)][:] for _ in group])],
+                local_sem=sem.sent)
+            left += _bits(m)
+        g.wait_ge(sem.sent, left)
+
+    srcs = []
+    for j in range(max(0, r - WINDOW), r):
+        cj = _calls(j, cores, topo)
+        n = [_bits(m) for m, group in cj if r in group][0]
+        nfar = sum(len(group) for m, group in cj if not _near(topo, cores[j], cores[group[0]]))
+        srcs.append((not _near(topo, cores[j], core), nfar, j, n))
+    srcs.sort()
+
+    t, v = g.tensor, g.vector
+    v.memset(T.zero[:, 0:W], 0.0).then_inc(sem.zf, 1)
+    v.wait_ge(sem.zf, 1)
+
+    t.wait_ge(sem.ldkv, 32)
+    t.wait_ge(sem.ldq, 16)
+    t.matmul(T.p0[:, 0:W], T.kv[:, 0:P], T.qs[:, 0:W], True, True).then_inc(sem.m0, 1)
+    v.wait_ge(sem.m0, 1)
+    v.tensor_tensor(T.s0[:, 0:W], T.p0[:, 0:W], T.zero[:, 0:W], AluOpType.max).then_inc(sem.r0, 1)
+    t.wait_ge(sem.r0, 1)
+    last = t.matmul(T.po[:, 0:W], T.kv[:, P:2 * P], T.s0[:, 0:W], True, not srcs)
+
+    for i, (far, nfar, j, n) in enumerate(srcs, 1):
+        ld = T["ld%d" % (j % 2)]
+        t.wait_ge(sem["arr%d" % (j % 2)], n)
+        t.matmul(T["p%d" % i][:, 0:W], ld[:, 0:P], T.qs[:, 0:W], True, True).then_inc(sem["m%d" % i], 1)
+        v.wait_ge(sem["m%d" % i], 1)
+        v.tensor_tensor(T["s%d" % i][:, 0:W], T["p%d" % i][:, 0:W], T.zero[:, 0:W],
+                        AluOpType.max).then_inc(sem["r%d" % i], 1)
+    for i, (far, nfar, j, n) in enumerate(srcs, 1):
+        ld = T["ld%d" % (j % 2)]
+        t.wait_ge(sem["r%d" % i], 1)
+        last = t.matmul(T.po[:, 0:W], ld[:, P:2 * P], T["s%d" % i][:, 0:W], False, i == len(srcs))
+    last.then_inc(sem.od, 1)
+
+    v.wait_ge(sem.od, 1)
+    v.tensor_copy(T.ys[:, 0:W], T.po[:, 0:W]).then_inc(sem.cp, 1)
+    g.sync.wait_ge(sem.cp, 1)
+    g.sync.dma_start(T.y[:, 0:W], T.ys[:, 0:W]).then_inc(sem.st, 16)
+    g.sync.wait_ge(sem.st, 16)

@@ -6,11 +6,13 @@ WINDOW = 2
 ENGINES = 8
 
 SCRATCH = {
-    "kv": ("sbuf", [P, 2 * P], "bfloat16"),
-    "ld0": ("sbuf", [P, 2 * P], "bfloat16"),
-    "ld1": ("sbuf", [P, 2 * P], "bfloat16"),
+    "ks": ("sbuf", [P, P], "bfloat16"),
+    "vs": ("sbuf", [P, P], "bfloat16"),
+    "lk0": ("sbuf", [P, P], "bfloat16"),
+    "lv0": ("sbuf", [P, P], "bfloat16"),
+    "lk1": ("sbuf", [P, P], "bfloat16"),
+    "lv1": ("sbuf", [P, P], "bfloat16"),
     "qs": ("sbuf", [P, P], "bfloat16"),
-    "zero": ("sbuf", [P, P], "float32"),
     "s0": ("sbuf", [P, P], "bfloat16"),
     "s1": ("sbuf", [P, P], "bfloat16"),
     "s2": ("sbuf", [P, P], "bfloat16"),
@@ -20,7 +22,7 @@ SCRATCH = {
     "p2": ("psum", [P, 512], "float32"),
     "po": ("psum", [P, 512], "float32"),
 }
-SEMAPHORES = ["ldkv", "ldq", "arr0", "arr1", "sent", "zf", "m0", "m1", "m2", "r0", "r1", "r2", "od", "cp", "st"]
+SEMAPHORES = ["ldk", "ldv", "ldq", "ak0", "ak1", "av0", "av1", "sent", "m0", "m1", "m2", "r0", "r1", "r2", "od", "cp", "st"]
 
 
 def _low(mask, n):
@@ -67,25 +69,28 @@ def rank_program(g, core, T, topo):
         return
     cores, sem = T.cores, T.sem
     W = T.tables["WID"][r]
+    par = r % 2
 
-    g.sync.dma_start(T.kv[:, 0:P], T.k[:, :]).then_inc(sem.ldkv, 16)
-    g.scalar.dma_start(T.kv[:, P:2 * P], T.v[:, :]).then_inc(sem.ldkv, 16)
+    g.sync.dma_start(T.ks[:, :], T.k[:, :]).then_inc(sem.ldk, 16)
+    g.scalar.dma_start(T.vs[:, :], T.v[:, :]).then_inc(sem.ldv, 16)
     g.sync.dma_start(T.qs[:, 0:W], T.q[:, 0:W]).then_inc(sem.ldq, 16)
 
     calls = _calls(r, cores, topo)
-    if calls:
-        g.wait_ge(sem.ldkv, 32)
-        left = 0
-        for m, group in calls:
-            ids = []
-            for d in group:
-                rid, pid = topo.addr(cores[d], core)
-                ids.append(DstId(rid=rid, pnc=pid))
+    left = 0
+    for c, (m, group) in enumerate(calls):
+        ids = []
+        for d in group:
+            rid, pid = topo.addr(cores[d], core)
+            ids.append(DstId(rid=rid, pnc=pid))
+        for own, land, arr, ld in ((T.ks, "lk", "ak", sem.ldk), (T.vs, "lv", "av", sem.ldv)):
+            if c == 0:
+                g.wait_ge(ld, 16)
             g.remote_dma_fused(
-                [RemoteDMATransfer(dst_ids=ids, dma_engine_mask=m, remote_sem=sem["arr%d" % (r % 2)],
-                                   srcs=[T.kv[:]], dsts=[T["ld%d" % (r % 2)][:] for _ in group])],
+                [RemoteDMATransfer(dst_ids=ids, dma_engine_mask=m, remote_sem=sem["%s%d" % (arr, par)],
+                                   srcs=[own[:]], dsts=[T["%s%d" % (land, par)][:] for _ in group])],
                 local_sem=sem.sent)
             left += _bits(m)
+    if calls:
         g.wait_ge(sem.sent, left)
 
     srcs = []
@@ -97,28 +102,24 @@ def rank_program(g, core, T, topo):
     srcs.sort()
 
     t, v = g.tensor, g.vector
-    v.memset(T.zero[:, 0:W], 0.0).then_inc(sem.zf, 1)
-    v.wait_ge(sem.zf, 1)
-
-    t.wait_ge(sem.ldkv, 32)
+    t.wait_ge(sem.ldk, 16)
     t.wait_ge(sem.ldq, 16)
-    t.matmul(T.p0[:, 0:W], T.kv[:, 0:P], T.qs[:, 0:W], True, True).then_inc(sem.m0, 1)
+    t.matmul(T.p0[:, 0:W], T.ks[:, :], T.qs[:, 0:W], True, True).then_inc(sem.m0, 1)
     v.wait_ge(sem.m0, 1)
-    v.tensor_tensor(T.s0[:, 0:W], T.p0[:, 0:W], T.zero[:, 0:W], AluOpType.max).then_inc(sem.r0, 1)
+    v.tensor_scalar(T.s0[:, 0:W], T.p0[:, 0:W], 0.0, None, AluOpType.max).then_inc(sem.r0, 1)
+    t.wait_ge(sem.ldv, 16)
     t.wait_ge(sem.r0, 1)
-    last = t.matmul(T.po[:, 0:W], T.kv[:, P:2 * P], T.s0[:, 0:W], True, not srcs)
+    last = t.matmul(T.po[:, 0:W], T.vs[:, :], T.s0[:, 0:W], True, not srcs)
 
     for i, (far, nfar, j, n) in enumerate(srcs, 1):
-        ld = T["ld%d" % (j % 2)]
-        t.wait_ge(sem["arr%d" % (j % 2)], n)
-        t.matmul(T["p%d" % i][:, 0:W], ld[:, 0:P], T.qs[:, 0:W], True, True).then_inc(sem["m%d" % i], 1)
+        t.wait_ge(sem["ak%d" % (j % 2)], n)
+        t.matmul(T["p%d" % i][:, 0:W], T["lk%d" % (j % 2)][:, :], T.qs[:, 0:W], True, True).then_inc(sem["m%d" % i], 1)
         v.wait_ge(sem["m%d" % i], 1)
-        v.tensor_tensor(T["s%d" % i][:, 0:W], T["p%d" % i][:, 0:W], T.zero[:, 0:W],
-                        AluOpType.max).then_inc(sem["r%d" % i], 1)
+        v.tensor_scalar(T["s%d" % i][:, 0:W], T["p%d" % i][:, 0:W], 0.0, None, AluOpType.max).then_inc(sem["r%d" % i], 1)
     for i, (far, nfar, j, n) in enumerate(srcs, 1):
-        ld = T["ld%d" % (j % 2)]
         t.wait_ge(sem["r%d" % i], 1)
-        last = t.matmul(T.po[:, 0:W], ld[:, P:2 * P], T["s%d" % i][:, 0:W], False, i == len(srcs))
+        t.wait_ge(sem["av%d" % (j % 2)], n)
+        last = t.matmul(T.po[:, 0:W], T["lv%d" % (j % 2)][:, :], T["s%d" % i][:, 0:W], False, i == len(srcs))
     last.then_inc(sem.od, 1)
 
     v.wait_ge(sem.od, 1)

from concourse.bass import DstId, RemoteDMATransfer
from concourse.mybir import AluOpType

P = 128
WINDOW = 2
ENGINES = 8

SCRATCH = {
    "ks": ("sbuf", [P, P], "bfloat16"),
    "vs": ("sbuf", [P, P], "bfloat16"),
    "lk0": ("sbuf", [P, P], "bfloat16"),
    "lv0": ("sbuf", [P, P], "bfloat16"),
    "lk1": ("sbuf", [P, P], "bfloat16"),
    "lv1": ("sbuf", [P, P], "bfloat16"),
    "qs": ("sbuf", [P, P], "bfloat16"),
    "s0": ("sbuf", [P, P], "bfloat16"),
    "s1": ("sbuf", [P, P], "bfloat16"),
    "s2": ("sbuf", [P, P], "bfloat16"),
    "ys": ("sbuf", [P, P], "bfloat16"),
    "p0": ("psum", [P, 512], "float32"),
    "p1": ("psum", [P, 512], "float32"),
    "p2": ("psum", [P, 512], "float32"),
    "po": ("psum", [P, 512], "float32"),
}
SEMAPHORES = ["ldk", "ldv", "ldq", "ak0", "ak1", "av0", "av1", "sent", "m0", "m1", "m2", "r0", "r1", "r2", "od", "cp", "st"]


def _low(mask, n):
    out, b = 0, 1
    while n and b <= mask:
        if mask & b:
            out |= b
            n -= 1
        b <<= 1
    return out


def _bits(mask):
    return bin(mask).count("1")


def _near(topo, a, b):
    return (topo.host(a), topo.chip(a)) == (topo.host(b), topo.chip(b))


def _calls(j, cores, topo):
    src = cores[j]
    dests = [d for d in range(j + 1, j + 1 + WINDOW) if d < len(cores)]
    far = [d for d in dests if not _near(topo, src, cores[d])]
    near = [d for d in dests if _near(topo, src, cores[d])]
    out, used = [], 0
    for group in (far, near):
        if not group:
            continue
        allowed = topo.mask(src, cores[group[0]])
        for d in group:
            assert topo.may_write(src, cores[d])
            allowed &= topo.mask(src, cores[d])
        free = allowed & ~used
        m = _low(free if _bits(free) >= ENGINES else allowed, ENGINES)
        used |= m
        out.append((m, group))
    return out


def rank_program(g, core, T, topo):
    r = T.rank_of(core)
    if r is None:
        return
    cores, sem = T.cores, T.sem
    W = T.tables["WID"][r]
    par = r % 2

    g.sync.dma_start(T.ks[:, :], T.k[:, :]).then_inc(sem.ldk, 16)
    g.scalar.dma_start(T.vs[:, :], T.v[:, :]).then_inc(sem.ldv, 16)
    g.sync.dma_start(T.qs[:, 0:W], T.q[:, 0:W]).then_inc(sem.ldq, 16)

    calls = _calls(r, cores, topo)
    left = 0
    for c, (m, group) in enumerate(calls):
        ids = []
        for d in group:
            rid, pid = topo.addr(cores[d], core)
            ids.append(DstId(rid=rid, pnc=pid))
        for own, land, arr, ld in ((T.ks, "lk", "ak", sem.ldk), (T.vs, "lv", "av", sem.ldv)):
            if c == 0:
                g.wait_ge(ld, 16)
            g.remote_dma_fused(
                [RemoteDMATransfer(dst_ids=ids, dma_engine_mask=m, remote_sem=sem["%s%d" % (arr, par)],
                                   srcs=[own[:]], dsts=[T["%s%d" % (land, par)][:] for _ in group])],
                local_sem=sem.sent)
            left += _bits(m)
    if calls:
        g.wait_ge(sem.sent, left)

    srcs = []
    for j in range(max(0, r - WINDOW), r):
        cj = _calls(j, cores, topo)
        n = [_bits(m) for m, group in cj if r in group][0]
        nfar = sum(len(group) for m, group in cj if not _near(topo, cores[j], cores[group[0]]))
        srcs.append((not _near(topo, cores[j], core), nfar, j, n))
    srcs.sort()

    t, v = g.tensor, g.vector
    t.wait_ge(sem.ldk, 16)
    t.wait_ge(sem.ldq, 16)
    t.matmul(T.p0[:, 0:W], T.ks[:, :], T.qs[:, 0:W], True, True).then_inc(sem.m0, 1)
    v.wait_ge(sem.m0, 1)
    v.tensor_scalar(T.s0[:, 0:W], T.p0[:, 0:W], 0.0, None, AluOpType.max).then_inc(sem.r0, 1)
    t.wait_ge(sem.ldv, 16)
    t.wait_ge(sem.r0, 1)
    last = t.matmul(T.po[:, 0:W], T.vs[:, :], T.s0[:, 0:W], True, not srcs)

    for i, (far, nfar, j, n) in enumerate(srcs, 1):
        t.wait_ge(sem["ak%d" % (j % 2)], n)
        t.matmul(T["p%d" % i][:, 0:W], T["lk%d" % (j % 2)][:, :], T.qs[:, 0:W], True, True).then_inc(sem["m%d" % i], 1)
        v.wait_ge(sem["m%d" % i], 1)
        v.tensor_scalar(T["s%d" % i][:, 0:W], T["p%d" % i][:, 0:W], 0.0, None, AluOpType.max).then_inc(sem["r%d" % i], 1)
    for i, (far, nfar, j, n) in enumerate(srcs, 1):
        t.wait_ge(sem["r%d" % i], 1)
        t.wait_ge(sem["av%d" % (j % 2)], n)
        last = t.matmul(T.po[:, 0:W], T["lv%d" % (j % 2)][:, :], T["s%d" % i][:, 0:W], False, i == len(srcs))
    last.then_inc(sem.od, 1)

    v.wait_ge(sem.od, 1)
    v.tensor_copy(T.ys[:, 0:W], T.po[:, 0:W]).then_inc(sem.cp, 1)
    g.sync.wait_ge(sem.cp, 1)
    g.sync.dma_start(T.y[:, 0:W], T.ys[:, 0:W]).then_inc(sem.st, 16)
    g.sync.wait_ge(sem.st, 16)
